import numpy as np
import ml_dtypes


def mxq(x, axis, fmt="e4m3"):
    dtype, down = {"e4m3": (ml_dtypes.float8_e4m3fn, 7), "e5m2": (ml_dtypes.float8_e5m2, 14)}[fmt]
    v = np.moveaxis(np.asarray(x, np.float32).astype(ml_dtypes.bfloat16).astype(np.float64), axis, -1)
    blocks = v.reshape(v.shape[:-1] + (-1, 32))
    amax = np.abs(blocks).max(-1, keepdims=True)
    byte = np.maximum(np.where(amax > 0, np.frexp(amax)[1] - 1 + 127, 0) - down, 1)
    scale = np.exp2(byte - 127.0)
    codes = (blocks / scale).astype(np.float32).astype(dtype).astype(np.float64)
    return np.moveaxis((codes * scale).reshape(v.shape), -1, axis)


WIDE = False


def mx_kscale(k):
    if not WIDE:
        return np.ones(k)
    levels = np.array([10, -10, 5, -5, 0])
    if k % 512:
        return np.exp2(np.random.permutation(np.resize(levels, k // 32))).repeat(32)
    a = np.empty((k // 512, 16))
    for p in range(k // 512):
        a[p, :8] = np.random.permutation(np.resize(levels, 8))
        for g in range(8):
            far = levels[np.abs(levels - a[p, g]) >= 10]
            a[p, g + 8] = far[np.random.randint(len(far))]
    return np.exp2(a.ravel()).repeat(32)


def f64(x):
    return np.asarray(x).astype(np.float64)


def striped(idx):
    return np.tile(idx.reshape(-1, 16).T, (8, 1)).astype(np.uint16)


def unstriped(offs):
    return offs[:16].T.reshape(-1).astype(np.int64)


def striped8(idx):
    return np.concatenate([x.reshape(-1, 16).T for x in idx]).astype(np.uint16)


def runs(offs, k):
    lists = np.stack([offs[16 * r : 16 * r + 16].T.reshape(-1) for r in range(8)]).astype(np.int64)
    return lists[np.arange(k) % 512 // 64]


def pack_weight(w):
    k, n = w.shape
    w = f64(np.asarray(w, np.float32).astype(ml_dtypes.bfloat16)).reshape(k // 32, 32, n)
    amax = np.abs(w).max(1)
    byte = np.clip(np.where(amax > 0, np.frexp(amax)[1] - 1 + 127 - 7, 1), 1, 254)
    scaled = (w * np.exp2(127.0 - byte)[:, None, :]).reshape(k, n).astype(np.float32)
    words = np.ascontiguousarray(scaled.reshape(k // 512, 128, 4, n).transpose(0, 1, 3, 2)).astype(ml_dtypes.float8_e4m3fn).view(np.uint8)
    return words, np.ascontiguousarray(byte.astype(np.uint8).reshape(k // 512, 16, n))


def unpack_weight(words, scales):
    g, p, n, _ = words.shape
    vals = np.ascontiguousarray(words).view(ml_dtypes.float8_e4m3fn).astype(np.float64) * np.repeat(np.exp2(scales.astype(np.float64) - 127.0), 8, axis=1)[..., None]
    return vals.transpose(0, 1, 3, 2).reshape(g * 512, n)


K, T, S, G, H, U = 512, 1024, 256, 2048, 512, 512


def setup_inputs():
    n = np.random.standard_normal
    s = mx_kscale(K)[:, None]
    packed_xT = pack_weight(n((K, T)) * s)
    packed_dT = pack_weight(n((K, G)) / s)
    perm = np.random.permutation(U)
    return {
        "x_words": packed_xT[0],
        "x_scales": packed_xT[1],
        "d_words": packed_dT[0],
        "d_scales": packed_dT[1],
        "gs": (np.random.uniform(0.5, 1.5, (K, 1)) * s).astype(np.float32),
        "offs": striped(np.random.permutation(T)[:S]),
        "k1": striped8(np.random.randint(0, G, (8, H))),
        "n1": striped(np.random.permutation(S)),
        "n2": striped(np.random.permutation(S)),
        "k2": striped8(np.random.randint(0, G, (8, H))),
        "k3": striped8(np.random.randint(0, G, (8, H))),
        "two": striped(np.random.permutation(T)[:S]),
        "n3": striped(perm[:S]),
        "n4": striped(perm[S:]),
        "n5": striped(np.random.permutation(S)),
    }


def reference(x_words, x_scales, d_words, d_scales, gs, offs, k1, n1, n2, k2, k3, two, n3, n4, n5):
    d_k2 = unpack_weight(d_words, d_scales)[np.arange(K)[:, None], runs(k2, K)]
    d_k1 = unpack_weight(d_words, d_scales)[np.arange(K)[:, None], runs(k1, K)]
    xq = unpack_weight(x_words, x_scales)[:, unstriped(offs)]
    h = 0.0625 * (d_k1.T @ xq)
    ds = np.zeros((H, S))
    ds[:, unstriped(n1)] = h
    st = np.maximum(h, ds)
    ds2 = np.zeros((H, S))
    ds2[:, unstriped(n2)] = st
    z = f64(gs) * (st - ds2)
    d_k3 = unpack_weight(d_words, d_scales)[np.arange(K)[:, None], runs(k3, K)]
    x_two = unpack_weight(x_words, x_scales)[:, unstriped(two)]
    h2 = 0.0625 * ((d_k2.T @ mxq(z, 0, "e4m3") + d_k3.T @ x_two))
    nw = h2 - h2[:, unstriped(n5)]
    ph = np.zeros((H, U))
    ph[:, unstriped(n3)] = h2
    out = ph.copy()
    out[:, unstriped(n4)] = nw
    return out

@@ -1,0 +1,203 @@
+from contextlib import ExitStack
+
+import concourse.mybir as mybir
+
+K, T, S, G, H, U = 512, 1024, 256, 2048, 512, 512
+FLOPS = 3 * 2 * K * H * S
+
+F32 = mybir.dt.float32
+BF16 = mybir.dt.bfloat16
+I32 = mybir.dt.int32
+U32 = mybir.dt.uint32
+U16 = mybir.dt.uint16
+U8 = mybir.dt.uint8
+FP8X4 = mybir.dt.float8_e4m3fn_x4
+ALU = mybir.AluOpType
+COPY = mybir.ActivationFunctionType.Copy
+
+P = 128
+PACK = 4
+TILES = H // P
+SPARE = 16
+ALIGN = 64
+SIXTEENTH = 0.0625
+
+
+def tile_picked_ctzmtsndtwinpagq_none_p_kernel(
+    tc, x_words, x_scales, d_words, d_scales, gs, offs, k1, n1, n2, k2, k3, two, n3, n4, n5, out
+):
+    nc = tc.nc
+    with ExitStack() as ctx:
+        lists = ctx.enter_context(tc.tile_pool(name="lists", bufs=1))
+        sb = ctx.enter_context(tc.tile_pool(name="sb", bufs=1))
+        psum = ctx.enter_context(tc.psum_pool(name="psum", bufs=1))
+
+        def sbuf(shape, dtype, name, tag=None):
+            return sb.tile(shape, dtype, name=name, tag=tag or name, align_bytes=ALIGN)
+
+        def load_list(src, name):
+            tile = lists.tile(list(src.shape), U16, name=name)
+            nc.sync.dma_start(tile[:], src)
+            return tile
+
+        def load_words(src, columns, name):
+            tile = sbuf([P, columns], U32, name)
+            nc.sync.dma_start(tile[:].bitcast(I32), src[0].rearrange("p n t -> p (n t)").bitcast(I32))
+            return tile
+
+        def load_scales(src, columns, name):
+            tile = sbuf([P, columns], U8, name)
+            nc.vector.memset(tile[:].bitcast(I32), 0)
+            nc.scalar.dma_start(tile[0:P:8, :].bitcast(I32), src[0].bitcast(I32))
+            return tile
+
+        def place_scale_rows(queue, placed, spread):
+            for r in range(4):
+                queue.dma_start(placed[r:P:32, :].bitcast(I32), spread[8 * r : P : 32, :].bitcast(I32))
+
+        def gather(dst, window, offsets):
+            nc.vector.tensor_copy(dst, window[:].indirect(offsets[:]))
+
+        def scatter(window, offsets, values):
+            nc.scalar.activation(window[:].indirect(offsets[:]), values, COPY)
+
+        d_scale_table = load_scales(d_scales, G, "d_scale_table")
+        x_scale_table = load_scales(x_scales, T, "x_scale_table")
+        k1_list = load_list(k1, "k1_list")
+        offs_list = load_list(offs, "offs_list")
+        d_word_table = load_words(d_words, G, "d_word_table")
+        x_word_table = load_words(x_words, T, "x_word_table")
+        n1_list = load_list(n1, "n1_list")
+        k3_list = load_list(k3, "k3_list")
+        k2_list = load_list(k2, "k2_list")
+        two_list = load_list(two, "two_list")
+        n2_list = load_list(n2, "n2_list")
+        n5_list = load_list(n5, "n5_list")
+        n3_list = load_list(n3, "n3_list")
+        n4_list = load_list(n4, "n4_list")
+        gs_rows = sbuf([P, PACK], F32, "gs_rows")
+        nc.gpsimd.dma_start(gs_rows[:], gs.rearrange("(p t) o -> p (t o)", t=PACK))
+        gain = sbuf([P, PACK], F32, "gain")
+        nc.scalar.activation(gain[:], gs_rows[:], COPY, scale=SIXTEENTH)
+
+        scales1 = sbuf([P, H + S], U8, "scales1")
+        nc.vector.memset(scales1[:].bitcast(I32), 0)
+        scales2 = sbuf([P, 2 * H + S], U8, "scales2")
+        nc.vector.memset(scales2[:].bitcast(I32), 0)
+        h2 = [sbuf([P, S + SPARE], F32, "h2_%d" % t) for t in range(TILES)]
+        for t in range(TILES):
+            nc.vector.memset(h2[t][:, S:], 0.0)
+
+        picked_scales1 = sbuf([P, H + S], U8, "picked_scales1")
+        dealt_scales1 = sbuf([P, H + S], U8, "dealt_scales1")
+        gather(picked_scales1[:, :H], d_scale_table, k1_list)
+        gather(picked_scales1[:, H:], x_scale_table, offs_list)
+        nc.vector.tensor_copy(
+            dealt_scales1[:, :H].rearrange("p (t m) -> p m t", t=PACK),
+            picked_scales1[:, :H].rearrange("p (m t) -> p m t", t=PACK),
+        )
+        nc.vector.tensor_copy(dealt_scales1[:, H:].bitcast(I32), picked_scales1[:, H:].bitcast(I32))
+        place_scale_rows(nc.scalar, scales1, dealt_scales1)
+
+        picked_k1 = sbuf([P, H], U32, "picked_k1")
+        dealt_k1 = sbuf([P, H], U32, "dealt_k1")
+        picked_x = sbuf([P, S], U32, "picked_x")
+        gather(picked_k1[:], d_word_table, k1_list)
+        gather(picked_x[:], x_word_table, offs_list)
+        nc.vector.tensor_copy(
+            dealt_k1[:].rearrange("p (t m) -> p m t", t=PACK),
+            picked_k1[:].rearrange("p (m t) -> p m t", t=PACK),
+        )
+
+        h_psum = [psum.tile([P, S], F32, name="h_psum%d" % t) for t in range(TILES)]
+        h = [sbuf([P, S], F32, "h_%d" % t) for t in range(TILES)]
+        for t in range(TILES):
+            rows = slice(t * P, (t + 1) * P)
+            nc.tensor.matmul_mx(
+                out=h_psum[t][:],
+                lhsT=dealt_k1[:, rows].bitcast(FP8X4),
+                lhsT_scale=scales1[:, rows],
+                rhs=picked_x[:].bitcast(FP8X4),
+                rhs_scale=scales1[:, H:],
+                start=True,
+                stop=True,
+            )
+        nc.scalar.activation(h[0][:], h_psum[0][:], COPY)
+        for t in range(1, TILES):
+            nc.vector.tensor_copy(h[t][:], h_psum[t][:])
+
+        ds = [sbuf([P, 2 * S], F32, "ds_%d" % t) for t in range(TILES)]
+        for t in range(TILES):
+            scatter(ds[t], n1_list, h[t][:])
+
+        picked_scales2 = sbuf([P, 2 * H + S], U8, "picked_scales2", tag="scales1")
+        picked2 = sbuf([P, 2 * H + S], U32, "picked2", tag="dealt_k1")
+        k3_cols, k2_cols, two_cols = slice(0, H), slice(H, 2 * H), slice(2 * H, 2 * H + S)
+        gather(picked_scales2[:, k3_cols], d_scale_table, k3_list)
+        gather(picked_scales2[:, k2_cols], d_scale_table, k2_list)
+        gather(picked_scales2[:, two_cols], x_scale_table, two_list)
+        place_scale_rows(nc.sync, scales2, picked_scales2)
+        gather(picked2[:, two_cols], x_word_table, two_list)
+        st_first = sbuf([P, S], F32, "st_first", tag="x_word_table")
+        nc.vector.tensor_tensor(st_first[:], h[0][:], ds[0][:, :S], ALU.max)
+        gather(picked2[:, k3_cols], d_word_table, k3_list)
+        gather(picked2[:, k2_cols], d_word_table, k2_list)
+        late = sbuf([P, 2 * TILES - 1, S], F32, "late", tag="d_word_table")
+        st = [st_first[:]] + [late[:, t - 1, :] for t in range(1, TILES)]
+        diff = [late[:, TILES - 1 + t, :] for t in range(TILES)]
+        for t in range(1, TILES):
+            nc.vector.tensor_tensor(st[t], h[t][:], ds[t][:, :S], ALU.max)
+
+        h2_psum = [psum.tile([P, S], F32, name="h2_psum%d" % t) for t in range(TILES)]
+        for t in range(TILES):
+            rows = slice(t * P, (t + 1) * P)
+            nc.tensor.matmul_mx(
+                out=h2_psum[t][:],
+                lhsT=picked2[:, rows].bitcast(FP8X4),
+                lhsT_scale=scales2[:, rows],
+                rhs=picked2[:, two_cols].bitcast(FP8X4),
+                rhs_scale=scales2[:, two_cols],
+                start=True,
+                stop=False,
+            )
+
+        ds2 = [sbuf([P, 2 * S], F32, "ds2_%d" % t) for t in range(TILES)]
+        z = sbuf([P, S, PACK], BF16, "z")
+        for t in range(TILES):
+            scatter(ds2[t], n2_list, st[t])
+            nc.vector.tensor_tensor(diff[t], st[t], ds2[t][:, :S], ALU.subtract)
+            nc.vector.tensor_scalar(z[:, :, t], diff[t], gain[:, t : t + 1], None, ALU.mult)
+        z_words = sbuf([P, S], U32, "z_words")
+        z_scales = sbuf([P, S], U8, "z_scales")
+        nc.vector.quantize_mx(z_words[:].bitcast(FP8X4), z_scales[:], z[:].rearrange("p c t -> p (c t)"))
+
+        for t in range(TILES):
+            rows = slice(H + t * P, H + (t + 1) * P)
+            nc.tensor.matmul_mx(
+                out=h2_psum[t][:],
+                lhsT=picked2[:, rows].bitcast(FP8X4),
+                lhsT_scale=scales2[:, rows],
+                rhs=z_words[:].bitcast(FP8X4),
+                rhs_scale=z_scales[:],
+                start=False,
+                stop=True,
+            )
+        nc.scalar.activation(h2[0][:, :S], h2_psum[0][:], COPY, scale=SIXTEENTH)
+        for t in range(1, TILES):
+            nc.vector.tensor_scalar(h2[t][:, :S], h2_psum[t][:], SIXTEENTH, None, ALU.mult)
+
+        page = [sbuf([P, U], F32, "page_%d" % t) for t in range(TILES)]
+        nw = [sbuf([P, S], F32, "nw_%d" % t) for t in range(TILES)]
+
+        def finish(t):
+            scatter(page[t], n4_list, nw[t][:])
+            nc.sync.dma_start(out[t * P : (t + 1) * P, :], page[t][:])
+
+        for t in range(TILES):
+            fetched = sbuf([P, S], F32, "fetched_%d" % t)
+            nc.scalar.activation(fetched[:], h2[t][:].indirect(n5_list[:]), COPY)
+            nc.vector.tensor_tensor(nw[t][:], h2[t][:, :S], fetched[:], ALU.subtract)
+            scatter(page[t], n3_list, h2[t][:, :S])
+            if t > 0:
+                finish(t - 1)
+        finish(TILES - 1)

@@ -45,15 +45,15 @@ def tile_picked_ctzmtsndtwinpagq_none_p_kernel(
             nc.sync.dma_start(tile[:].bitcast(I32), src[0].rearrange("p n t -> p (n t)").bitcast(I32))
             return tile
 
-        def load_scales(src, columns, name):
+        def load_scales(clearer, queue, src, columns, name):
             tile = sbuf([P, columns], U8, name)
-            nc.vector.memset(tile[:].bitcast(I32), 0)
-            nc.scalar.dma_start(tile[0:P:8, :].bitcast(I32), src[0].bitcast(I32))
+            clearer.memset(tile[:].bitcast(I32), 0)
+            queue.dma_start(tile[0:P:8, :].bitcast(I32), src[0].bitcast(I32))
             return tile
 
-        def place_scale_rows(queue, placed, spread):
+        def place_scale_rows(placed, spread):
             for r in range(4):
-                queue.dma_start(placed[r:P:32, :].bitcast(I32), spread[8 * r : P : 32, :].bitcast(I32))
+                nc.sync.dma_start(placed[r:P:32, :].bitcast(I32), spread[8 * r : P : 32, :].bitcast(I32))
 
         def gather(dst, window, offsets):
             nc.vector.tensor_copy(dst, window[:].indirect(offsets[:]))
@@ -61,32 +61,33 @@ def tile_picked_ctzmtsndtwinpagq_none_p_kernel(
         def scatter(window, offsets, values):
             nc.scalar.activation(window[:].indirect(offsets[:]), values, COPY)
 
-        d_scale_table = load_scales(d_scales, G, "d_scale_table")
-        x_scale_table = load_scales(x_scales, T, "x_scale_table")
+        h2 = [sbuf([P, S + SPARE], F32, "h2_%d" % t) for t in range(TILES)]
+        zeros = sbuf([P, SPARE], F32, "zeros", tag="d_word_table")
+        nc.vector.memset(zeros[:], 0.0)
+        d_scale_table = load_scales(nc.vector, nc.scalar, d_scales, G, "d_scale_table")
+        nc.vector.tensor_copy(h2[0][:, S:], zeros[:])
+        x_scale_table = load_scales(nc.gpsimd, nc.sync, x_scales, T, "x_scale_table")
         k1_list = load_list(k1, "k1_list")
         offs_list = load_list(offs, "offs_list")
         d_word_table = load_words(d_words, G, "d_word_table")
-        x_word_table = load_words(x_words, T, "x_word_table")
         n1_list = load_list(n1, "n1_list")
         k3_list = load_list(k3, "k3_list")
         k2_list = load_list(k2, "k2_list")
         two_list = load_list(two, "two_list")
-        n2_list = load_list(n2, "n2_list")
-        n5_list = load_list(n5, "n5_list")
-        n3_list = load_list(n3, "n3_list")
-        n4_list = load_list(n4, "n4_list")
         gs_rows = sbuf([P, PACK], F32, "gs_rows")
-        nc.gpsimd.dma_start(gs_rows[:], gs.rearrange("(p t) o -> p (t o)", t=PACK))
-        gain = sbuf([P, PACK], F32, "gain")
-        nc.scalar.activation(gain[:], gs_rows[:], COPY, scale=SIXTEENTH)
+        nc.sync.dma_start(gs_rows[:], gs.rearrange("(p t) o -> p (t o)", t=PACK))
+        n2_list = load_list(n2, "n2_list")
+        x_word_table = load_words(x_words, T, "x_word_table")
 
         scales1 = sbuf([P, H + S], U8, "scales1")
         nc.vector.memset(scales1[:].bitcast(I32), 0)
         scales2 = sbuf([P, 2 * H + S], U8, "scales2")
         nc.vector.memset(scales2[:].bitcast(I32), 0)
-        h2 = [sbuf([P, S + SPARE], F32, "h2_%d" % t) for t in range(TILES)]
-        for t in range(TILES):
+        for t in range(1, TILES):
             nc.vector.memset(h2[t][:, S:], 0.0)
+
+        sixteenth = sbuf([P, 1], F32, "sixteenth")
+        nc.vector.memset(sixteenth[:], SIXTEENTH)
 
         picked_scales1 = sbuf([P, H + S], U8, "picked_scales1")
         dealt_scales1 = sbuf([P, H + S], U8, "dealt_scales1")
@@ -97,7 +98,10 @@ def tile_picked_ctzmtsndtwinpagq_none_p_kernel(
             picked_scales1[:, :H].rearrange("p (m t) -> p m t", t=PACK),
         )
         nc.vector.tensor_copy(dealt_scales1[:, H:].bitcast(I32), picked_scales1[:, H:].bitcast(I32))
-        place_scale_rows(nc.scalar, scales1, dealt_scales1)
+        place_scale_rows(scales1, dealt_scales1)
+        n5_list = load_list(n5, "n5_list")
+        n3_list = load_list(n3, "n3_list")
+        n4_list = load_list(n4, "n4_list")
 
         picked_k1 = sbuf([P, H], U32, "picked_k1")
         dealt_k1 = sbuf([P, H], U32, "dealt_k1")
@@ -122,30 +126,32 @@ def tile_picked_ctzmtsndtwinpagq_none_p_kernel(
                 start=True,
                 stop=True,
             )
-        nc.scalar.activation(h[0][:], h_psum[0][:], COPY)
+        nc.scalar.activation(h[0][:], h_psum[0][:], COPY, scale=SIXTEENTH)
         for t in range(1, TILES):
-            nc.vector.tensor_copy(h[t][:], h_psum[t][:])
+            nc.vector.tensor_scalar(h[t][:], h_psum[t][:], sixteenth[:], None, ALU.mult)
 
         ds = [sbuf([P, 2 * S], F32, "ds_%d" % t) for t in range(TILES)]
         for t in range(TILES):
             scatter(ds[t], n1_list, h[t][:])
 
-        picked_scales2 = sbuf([P, 2 * H + S], U8, "picked_scales2", tag="scales1")
-        picked2 = sbuf([P, 2 * H + S], U32, "picked2", tag="dealt_k1")
-        k3_cols, k2_cols, two_cols = slice(0, H), slice(H, 2 * H), slice(2 * H, 2 * H + S)
-        gather(picked_scales2[:, k3_cols], d_scale_table, k3_list)
-        gather(picked_scales2[:, k2_cols], d_scale_table, k2_list)
-        gather(picked_scales2[:, two_cols], x_scale_table, two_list)
-        place_scale_rows(nc.sync, scales2, picked_scales2)
-        gather(picked2[:, two_cols], x_word_table, two_list)
-        st_first = sbuf([P, S], F32, "st_first", tag="x_word_table")
-        nc.vector.tensor_tensor(st_first[:], h[0][:], ds[0][:, :S], ALU.max)
-        gather(picked2[:, k3_cols], d_word_table, k3_list)
-        gather(picked2[:, k2_cols], d_word_table, k2_list)
-        late = sbuf([P, 2 * TILES - 1, S], F32, "late", tag="d_word_table")
-        st = [st_first[:]] + [late[:, t - 1, :] for t in range(1, TILES)]
-        diff = [late[:, TILES - 1 + t, :] for t in range(TILES)]
-        for t in range(1, TILES):
+        picked_scales2 = sbuf([P, 2 * H + S], U8, "picked_scales2", tag="sixteenth")
+        gather(picked_scales2[:, :H], d_scale_table, k3_list)
+        gather(picked_scales2[:, H : 2 * H], d_scale_table, k2_list)
+        gather(picked_scales2[:, 2 * H :], x_scale_table, two_list)
+        place_scale_rows(scales2, picked_scales2)
+        picked_two = sbuf([P, S], U32, "picked_two", tag="x_scale_table")
+        gather(picked_two[:], x_word_table, two_list)
+        early = sbuf([P, 2, S], F32, "early", tag="x_word_table")
+        st = [early[:, 0, :], early[:, 1, :]]
+        for t in range(2):
+            nc.vector.tensor_tensor(st[t], h[t][:], ds[t][:, :S], ALU.max)
+        picked2 = sbuf([P, 2 * H], U32, "picked2", tag="ds_1")
+        gather(picked2[:, :H], d_word_table, k3_list)
+        gather(picked2[:, H:], d_word_table, k2_list)
+        late = sbuf([P, 2 + TILES, S], F32, "late", tag="d_word_table")
+        st = st + [late[:, 0, :], late[:, 1, :]]
+        diff = [late[:, 2 + t, :] for t in range(TILES)]
+        for t in range(2, TILES):
             nc.vector.tensor_tensor(st[t], h[t][:], ds[t][:, :S], ALU.max)
 
         h2_psum = [psum.tile([P, S], F32, name="h2_psum%d" % t) for t in range(TILES)]
@@ -155,8 +161,8 @@ def tile_picked_ctzmtsndtwinpagq_none_p_kernel(
                 out=h2_psum[t][:],
                 lhsT=picked2[:, rows].bitcast(FP8X4),
                 lhsT_scale=scales2[:, rows],
-                rhs=picked2[:, two_cols].bitcast(FP8X4),
-                rhs_scale=scales2[:, two_cols],
+                rhs=picked_two[:].bitcast(FP8X4),
+                rhs_scale=scales2[:, 2 * H :],
                 start=True,
                 stop=False,
             )
@@ -166,7 +172,7 @@ def tile_picked_ctzmtsndtwinpagq_none_p_kernel(
         for t in range(TILES):
             scatter(ds2[t], n2_list, st[t])
             nc.vector.tensor_tensor(diff[t], st[t], ds2[t][:, :S], ALU.subtract)
-            nc.vector.tensor_scalar(z[:, :, t], diff[t], gain[:, t : t + 1], None, ALU.mult)
+            nc.vector.tensor_scalar(z[:, :, t], diff[t], gs_rows[:, t : t + 1], None, ALU.mult)
         z_words = sbuf([P, S], U32, "z_words")
         z_scales = sbuf([P, S], U8, "z_scales")
         nc.vector.quantize_mx(z_words[:].bitcast(FP8X4), z_scales[:], z[:].rearrange("p c t -> p (c t)"))

@@ -59,7 +59,7 @@ def tile_picked_ctzmtsndtwinpagq_none_p_kernel(
             nc.vector.tensor_copy(dst, window[:].indirect(offsets[:]))
 
         def scatter(window, offsets, values):
-            nc.scalar.activation(window[:].indirect(offsets[:]), values, COPY)
+            nc.scalar.activation(window[:].indirect(offsets), values, COPY)
 
         h2 = [sbuf([P, S + SPARE], F32, "h2_%d" % t) for t in range(TILES)]
         zeros = sbuf([P, SPARE], F32, "zeros", tag="d_word_table")
@@ -132,7 +132,7 @@ def tile_picked_ctzmtsndtwinpagq_none_p_kernel(
 
         ds = [sbuf([P, 2 * S], F32, "ds_%d" % t) for t in range(TILES)]
         for t in range(TILES):
-            scatter(ds[t], n1_list, h[t][:])
+            scatter(ds[t], n1_list[:], h[t][:])
 
         picked_scales2 = sbuf([P, 2 * H + S], U8, "picked_scales2", tag="sixteenth")
         gather(picked_scales2[:, :H], d_scale_table, k3_list)
@@ -154,56 +154,70 @@ def tile_picked_ctzmtsndtwinpagq_none_p_kernel(
         for t in range(2, TILES):
             nc.vector.tensor_tensor(st[t], h[t][:], ds[t][:, :S], ALU.max)
 
-        h2_psum = [psum.tile([P, S], F32, name="h2_psum%d" % t) for t in range(TILES)]
-        for t in range(TILES):
+        halves = [slice(0, S // 2), slice(S // 2, S)]
+        pieces = [(0, cols) for cols in halves] + [(t, slice(0, S)) for t in range(1, TILES)]
+        banks = ["h2_psum0", "h_psum0", "h2_psum1", "h2_psum2", "h2_psum3"]
+        h2_psum = [
+            psum.tile([P, cols.stop - cols.start], F32, name="h2_psum_%d" % i, tag=banks[i])
+            for i, (t, cols) in enumerate(pieces)
+        ]
+        for i, (t, cols) in enumerate(pieces):
             rows = slice(t * P, (t + 1) * P)
             nc.tensor.matmul_mx(
-                out=h2_psum[t][:],
+                out=h2_psum[i][:],
                 lhsT=picked2[:, rows].bitcast(FP8X4),
                 lhsT_scale=scales2[:, rows],
-                rhs=picked_two[:].bitcast(FP8X4),
-                rhs_scale=scales2[:, 2 * H :],
+                rhs=picked_two[:, cols].bitcast(FP8X4),
+                rhs_scale=scales2[:, 2 * H :][:, cols],
                 start=True,
                 stop=False,
             )
 
         ds2 = [sbuf([P, 2 * S], F32, "ds2_%d" % t) for t in range(TILES)]
         z = sbuf([P, S, PACK], BF16, "z")
-        for t in range(TILES):
-            scatter(ds2[t], n2_list, st[t])
-            nc.vector.tensor_tensor(diff[t], st[t], ds2[t][:, :S], ALU.subtract)
-            nc.vector.tensor_scalar(z[:, :, t], diff[t], gs_rows[:, t : t + 1], None, ALU.mult)
         z_words = sbuf([P, S], U32, "z_words")
         z_scales = sbuf([P, S], U8, "z_scales")
-        nc.vector.quantize_mx(z_words[:].bitcast(FP8X4), z_scales[:], z[:].rearrange("p c t -> p (c t)"))
-
         for t in range(TILES):
+            scatter(ds2[t], n2_list[:], st[t])
+            for cols in halves if t == TILES - 1 else [slice(0, S)]:
+                nc.vector.tensor_tensor(diff[t][:, cols], st[t][:, cols], ds2[t][:, cols], ALU.subtract)
+                nc.vector.tensor_scalar(z[:, cols, t], diff[t][:, cols], gs_rows[:, t : t + 1], None, ALU.mult)
+        for cols in halves:
+            nc.vector.quantize_mx(
+                z_words[:, cols].bitcast(FP8X4), z_scales[:, cols], z[:, cols, :].rearrange("p c t -> p (c t)")
+            )
+
+        for i, (t, cols) in enumerate(pieces):
             rows = slice(H + t * P, H + (t + 1) * P)
             nc.tensor.matmul_mx(
-                out=h2_psum[t][:],
+                out=h2_psum[i][:],
                 lhsT=picked2[:, rows].bitcast(FP8X4),
                 lhsT_scale=scales2[:, rows],
-                rhs=z_words[:].bitcast(FP8X4),
-                rhs_scale=z_scales[:],
+                rhs=z_words[:, cols].bitcast(FP8X4),
+                rhs_scale=z_scales[:, cols],
                 start=False,
                 stop=True,
             )
-        nc.scalar.activation(h2[0][:, :S], h2_psum[0][:], COPY, scale=SIXTEENTH)
-        for t in range(1, TILES):
-            nc.vector.tensor_scalar(h2[t][:, :S], h2_psum[t][:], SIXTEENTH, None, ALU.mult)
+        nc.scalar.activation(h2[0][:, halves[0]], h2_psum[0][:], COPY, scale=SIXTEENTH)
+        for i, (t, cols) in list(enumerate(pieces))[1:]:
+            nc.vector.tensor_scalar(h2[t][:, cols], h2_psum[i][:], SIXTEENTH, None, ALU.mult)
 
         page = [sbuf([P, U], F32, "page_%d" % t) for t in range(TILES)]
         nw = [sbuf([P, S], F32, "nw_%d" % t) for t in range(TILES)]
 
         def finish(t):
-            scatter(page[t], n4_list, nw[t][:])
+            scatter(page[t], n4_list[:], nw[t][:])
             nc.sync.dma_start(out[t * P : (t + 1) * P, :], page[t][:])
 
+        half_list = S // 2 // 16
+        scatter(page[0], n3_list[:, :half_list], h2[0][:, halves[0]])
         for t in range(TILES):
             fetched = sbuf([P, S], F32, "fetched_%d" % t)
             nc.scalar.activation(fetched[:], h2[t][:].indirect(n5_list[:]), COPY)
             nc.vector.tensor_tensor(nw[t][:], h2[t][:, :S], fetched[:], ALU.subtract)
-            scatter(page[t], n3_list, h2[t][:, :S])
-            if t > 0:
+            if t == 0:
+                scatter(page[0], n3_list[:, half_list:], h2[0][:, halves[1]])
+            else:
+                scatter(page[t], n3_list[:], h2[t][:, :S])
                 finish(t - 1)
         finish(TILES - 1)

@@ -51,12 +51,12 @@ def tile_picked_ctzmtsndtwinpagq_none_p_kernel(
             queue.dma_start(tile[0:P:8, :].bitcast(I32), src[0].bitcast(I32))
             return tile
 
-        def place_scale_rows(placed, spread):
-            for r in range(4):
+        def place_scale_rows(placed, spread, which):
+            for r in which:
                 nc.sync.dma_start(placed[r:P:32, :].bitcast(I32), spread[8 * r : P : 32, :].bitcast(I32))
 
         def gather(dst, window, offsets):
-            nc.vector.tensor_copy(dst, window[:].indirect(offsets[:]))
+            nc.vector.tensor_copy(dst, window[:].indirect(offsets))
 
         def scatter(window, offsets, values):
             nc.scalar.activation(window[:].indirect(offsets), values, COPY)
@@ -79,8 +79,6 @@ def tile_picked_ctzmtsndtwinpagq_none_p_kernel(
         n2_list = load_list(n2, "n2_list")
         x_word_table = load_words(x_words, T, "x_word_table")
 
-        scales1 = sbuf([P, H + S], U8, "scales1")
-        nc.vector.memset(scales1[:].bitcast(I32), 0)
         scales2 = sbuf([P, 2 * H + S], U8, "scales2")
         nc.vector.memset(scales2[:].bitcast(I32), 0)
         for t in range(1, TILES):
@@ -90,15 +88,15 @@ def tile_picked_ctzmtsndtwinpagq_none_p_kernel(
         nc.vector.memset(sixteenth[:], SIXTEENTH)
 
         picked_scales1 = sbuf([P, H + S], U8, "picked_scales1")
-        dealt_scales1 = sbuf([P, H + S], U8, "dealt_scales1")
-        gather(picked_scales1[:, :H], d_scale_table, k1_list)
-        gather(picked_scales1[:, H:], x_scale_table, offs_list)
+        scales1 = sbuf([P, H + S], U8, "scales1")
+        gather(picked_scales1[:, :H], d_scale_table, k1_list[:])
+        gather(picked_scales1[:, H:], x_scale_table, offs_list[:])
         nc.vector.tensor_copy(
-            dealt_scales1[:, :H].rearrange("p (t m) -> p m t", t=PACK),
+            scales1[:, :H].rearrange("p (t m) -> p m t", t=PACK),
             picked_scales1[:, :H].rearrange("p (m t) -> p m t", t=PACK),
         )
-        nc.vector.tensor_copy(dealt_scales1[:, H:].bitcast(I32), picked_scales1[:, H:].bitcast(I32))
-        place_scale_rows(scales1, dealt_scales1)
+        nc.vector.tensor_copy(scales1[:, H:].bitcast(I32), picked_scales1[:, H:].bitcast(I32))
+        place_scale_rows(scales1, scales1, range(1, 4))
         n5_list = load_list(n5, "n5_list")
         n3_list = load_list(n3, "n3_list")
         n4_list = load_list(n4, "n4_list")
@@ -106,57 +104,64 @@ def tile_picked_ctzmtsndtwinpagq_none_p_kernel(
         picked_k1 = sbuf([P, H], U32, "picked_k1")
         dealt_k1 = sbuf([P, H], U32, "dealt_k1")
         picked_x = sbuf([P, S], U32, "picked_x")
-        gather(picked_k1[:], d_word_table, k1_list)
-        gather(picked_x[:], x_word_table, offs_list)
-        nc.vector.tensor_copy(
-            dealt_k1[:].rearrange("p (t m) -> p m t", t=PACK),
-            picked_k1[:].rearrange("p (m t) -> p m t", t=PACK),
-        )
+        halves = [slice(0, S // 2), slice(S // 2, S)]
+        whole = slice(0, S)
+        half_list = S // 2 // 16
 
-        h_psum = [psum.tile([P, S], F32, name="h_psum%d" % t) for t in range(TILES)]
+        def entries(offsets, cols):
+            return offsets[:, cols.start // 16 : cols.stop // 16]
+
+        gather(picked_k1[:], d_word_table, k1_list[:])
+        by_tile = picked_k1[:].rearrange("p (m t) -> p m t", t=PACK)
+        gather(picked_x[:, halves[0]], x_word_table, entries(offs_list, halves[0]))
+        nc.vector.tensor_copy(dealt_k1[:, :P], by_tile[:, :, 0])
+        gather(picked_x[:, halves[1]], x_word_table, entries(offs_list, halves[1]))
+        nc.vector.tensor_copy(dealt_k1[:, P:].rearrange("p (t m) -> p m t", t=PACK - 1), by_tile[:, :, 1:])
+
+        pieces1 = [(0, halves[0]), (1, whole), (0, halves[1]), (2, whole), (3, whole)]
         h = [sbuf([P, S], F32, "h_%d" % t) for t in range(TILES)]
-        for t in range(TILES):
+        ds = [sbuf([P, 2 * S], F32, "ds_%d" % t) for t in range(TILES)]
+        for i, (t, cols) in enumerate(pieces1):
             rows = slice(t * P, (t + 1) * P)
+            acc = psum.tile([P, cols.stop - cols.start], F32, name="h_psum%d" % i, tag="bank%d" % i)
             nc.tensor.matmul_mx(
-                out=h_psum[t][:],
+                out=acc[:],
                 lhsT=dealt_k1[:, rows].bitcast(FP8X4),
                 lhsT_scale=scales1[:, rows],
-                rhs=picked_x[:].bitcast(FP8X4),
-                rhs_scale=scales1[:, H:],
+                rhs=picked_x[:, cols].bitcast(FP8X4),
+                rhs_scale=scales1[:, H:][:, cols],
                 start=True,
                 stop=True,
             )
-        nc.scalar.activation(h[0][:], h_psum[0][:], COPY, scale=SIXTEENTH)
-        for t in range(1, TILES):
-            nc.vector.tensor_scalar(h[t][:], h_psum[t][:], sixteenth[:], None, ALU.mult)
-
-        ds = [sbuf([P, 2 * S], F32, "ds_%d" % t) for t in range(TILES)]
-        for t in range(TILES):
-            scatter(ds[t], n1_list[:], h[t][:])
+            if i == 0:
+                nc.scalar.activation(h[t][:, cols], acc[:], COPY, scale=SIXTEENTH)
+            else:
+                nc.vector.tensor_scalar(h[t][:, cols], acc[:], sixteenth[:], None, ALU.mult)
+        for t, cols in pieces1:
+            scatter(ds[t], entries(n1_list, cols), h[t][:, cols])
 
         picked_scales2 = sbuf([P, 2 * H + S], U8, "picked_scales2", tag="sixteenth")
-        gather(picked_scales2[:, :H], d_scale_table, k3_list)
-        gather(picked_scales2[:, H : 2 * H], d_scale_table, k2_list)
-        gather(picked_scales2[:, 2 * H :], x_scale_table, two_list)
-        place_scale_rows(scales2, picked_scales2)
+        gather(picked_scales2[:, :H], d_scale_table, k3_list[:])
+        gather(picked_scales2[:, H : 2 * H], d_scale_table, k2_list[:])
+        gather(picked_scales2[:, 2 * H :], x_scale_table, two_list[:])
+        place_scale_rows(scales2, picked_scales2, range(4))
         picked_two = sbuf([P, S], U32, "picked_two", tag="x_scale_table")
-        gather(picked_two[:], x_word_table, two_list)
+        gather(picked_two[:], x_word_table, two_list[:])
         early = sbuf([P, 2, S], F32, "early", tag="x_word_table")
         st = [early[:, 0, :], early[:, 1, :]]
         for t in range(2):
             nc.vector.tensor_tensor(st[t], h[t][:], ds[t][:, :S], ALU.max)
         picked2 = sbuf([P, 2 * H], U32, "picked2", tag="ds_1")
-        gather(picked2[:, :H], d_word_table, k3_list)
-        gather(picked2[:, H:], d_word_table, k2_list)
+        gather(picked2[:, :H], d_word_table, k3_list[:])
+        gather(picked2[:, H:], d_word_table, k2_list[:])
         late = sbuf([P, 2 + TILES, S], F32, "late", tag="d_word_table")
         st = st + [late[:, 0, :], late[:, 1, :]]
         diff = [late[:, 2 + t, :] for t in range(TILES)]
         for t in range(2, TILES):
             nc.vector.tensor_tensor(st[t], h[t][:], ds[t][:, :S], ALU.max)
 
-        halves = [slice(0, S // 2), slice(S // 2, S)]
         pieces = [(0, cols) for cols in halves] + [(t, slice(0, S)) for t in range(1, TILES)]
-        banks = ["h2_psum0", "h_psum0", "h2_psum1", "h2_psum2", "h2_psum3"]
+        banks = ["bank5", "bank6", "bank7", "bank0", "bank1"]
         h2_psum = [
             psum.tile([P, cols.stop - cols.start], F32, name="h2_psum_%d" % i, tag=banks[i])
             for i, (t, cols) in enumerate(pieces)
@@ -209,7 +214,6 @@ def tile_picked_ctzmtsndtwinpagq_none_p_kernel(
             scatter(page[t], n4_list[:], nw[t][:])
             nc.sync.dma_start(out[t * P : (t + 1) * P, :], page[t][:])
 
-        half_list = S // 2 // 16
         scatter(page[0], n3_list[:, :half_list], h2[0][:, halves[0]])
         for t in range(TILES):
             fetched = sbuf([P, S], F32, "fetched_%d" % t)

@@ -76,6 +76,8 @@ def tile_picked_ctzmtsndtwinpagq_none_p_kernel(
         two_list = load_list(two, "two_list")
         gs_rows = sbuf([P, PACK], F32, "gs_rows")
         nc.sync.dma_start(gs_rows[:], gs.rearrange("(p t) o -> p (t o)", t=PACK))
+        minus_gs = sbuf([P, PACK], F32, "minus_gs")
+        nc.gpsimd.tensor_scalar(minus_gs[:], gs_rows[:], -1.0, 0.0, ALU.mult, ALU.add)
         n2_list = load_list(n2, "n2_list")
         x_word_table = load_words(x_words, T, "x_word_table")
 
@@ -184,9 +186,11 @@ def tile_picked_ctzmtsndtwinpagq_none_p_kernel(
         z_scales = sbuf([P, S], U8, "z_scales")
         for t in range(TILES):
             scatter(ds2[t], n2_list[:], st[t])
-            for cols in halves if t == TILES - 1 else [slice(0, S)]:
-                nc.vector.tensor_tensor(diff[t][:, cols], st[t][:, cols], ds2[t][:, cols], ALU.subtract)
-                nc.vector.tensor_scalar(z[:, cols, t], diff[t][:, cols], gs_rows[:, t : t + 1], None, ALU.mult)
+            nc.vector.tensor_scalar(diff[t], st[t], minus_gs[:, t : t + 1], None, ALU.mult)
+            for cols in halves if t == TILES - 1 else [whole]:
+                nc.vector.scalar_tensor_tensor(
+                    z[:, cols, t], ds2[t][:, cols], minus_gs[:, t : t + 1], diff[t][:, cols], ALU.mult, ALU.subtract
+                )
         for cols in halves:
             nc.vector.quantize_mx(
                 z_words[:, cols].bitcast(FP8X4), z_scales[:, cols], z[:, cols, :].rearrange("p c t -> p (c t)")

from contextlib import ExitStack

import concourse.mybir as mybir

K, T, S, G, H, U = 512, 1024, 256, 2048, 512, 512
FLOPS = 3 * 2 * K * H * S

F32 = mybir.dt.float32
BF16 = mybir.dt.bfloat16
I32 = mybir.dt.int32
U32 = mybir.dt.uint32
U16 = mybir.dt.uint16
U8 = mybir.dt.uint8
FP8X4 = mybir.dt.float8_e4m3fn_x4
ALU = mybir.AluOpType
COPY = mybir.ActivationFunctionType.Copy

P = 128
PACK = 4
TILES = H // P
SPARE = 16
ALIGN = 64
SIXTEENTH = 0.0625


def tile_picked_ctzmtsndtwinpagq_none_p_kernel(
    tc, x_words, x_scales, d_words, d_scales, gs, offs, k1, n1, n2, k2, k3, two, n3, n4, n5, out
):
    nc = tc.nc
    with ExitStack() as ctx:
        lists = ctx.enter_context(tc.tile_pool(name="lists", bufs=1))
        sb = ctx.enter_context(tc.tile_pool(name="sb", bufs=1))
        psum = ctx.enter_context(tc.psum_pool(name="psum", bufs=1))

        def sbuf(shape, dtype, name, tag=None):
            return sb.tile(shape, dtype, name=name, tag=tag or name, align_bytes=ALIGN)

        def load_list(src, name):
            tile = lists.tile(list(src.shape), U16, name=name)
            nc.sync.dma_start(tile[:], src)
            return tile

        def load_words(src, columns, name):
            tile = sbuf([P, columns], U32, name)
            nc.sync.dma_start(tile[:].bitcast(I32), src[0].rearrange("p n t -> p (n t)").bitcast(I32))
            return tile

        def load_scales(clearer, queue, src, columns, name):
            tile = sbuf([P, columns], U8, name)
            clearer.memset(tile[:].bitcast(I32), 0)
            queue.dma_start(tile[0:P:8, :].bitcast(I32), src[0].bitcast(I32))
            return tile

        def place_scale_rows(placed, spread, which):
            for r in which:
                nc.sync.dma_start(placed[r:P:32, :].bitcast(I32), spread[8 * r : P : 32, :].bitcast(I32))

        def gather(dst, window, offsets):
            nc.vector.tensor_copy(dst, window[:].indirect(offsets))

        def scatter(window, offsets, values):
            nc.scalar.activation(window[:].indirect(offsets), values, COPY)

        h2 = [sbuf([P, S + SPARE], F32, "h2_%d" % t) for t in range(TILES)]
        zeros = sbuf([P, SPARE], F32, "zeros", tag="d_word_table")
        nc.vector.memset(zeros[:], 0.0)
        d_scale_table = load_scales(nc.vector, nc.scalar, d_scales, G, "d_scale_table")
        nc.vector.tensor_copy(h2[0][:, S:], zeros[:])
        x_scale_table = load_scales(nc.gpsimd, nc.sync, x_scales, T, "x_scale_table")
        k1_list = load_list(k1, "k1_list")
        offs_list = load_list(offs, "offs_list")
        d_word_table = load_words(d_words, G, "d_word_table")
        n1_list = load_list(n1, "n1_list")
        k3_list = load_list(k3, "k3_list")
        k2_list = load_list(k2, "k2_list")
        two_list = load_list(two, "two_list")
        gs_rows = sbuf([P, PACK], F32, "gs_rows")
        nc.sync.dma_start(gs_rows[:], gs.rearrange("(p t) o -> p (t o)", t=PACK))
        minus_gs = sbuf([P, PACK], F32, "minus_gs")
        nc.gpsimd.tensor_scalar(minus_gs[:], gs_rows[:], -1.0, 0.0, ALU.mult, ALU.add)
        n2_list = load_list(n2, "n2_list")
        x_word_table = load_words(x_words, T, "x_word_table")

        scales2 = sbuf([P, 2 * H + S], U8, "scales2")
        nc.vector.memset(scales2[:].bitcast(I32), 0)
        for t in range(1, TILES):
            nc.vector.memset(h2[t][:, S:], 0.0)

        sixteenth = sbuf([P, 1], F32, "sixteenth")
        nc.vector.memset(sixteenth[:], SIXTEENTH)

        picked_scales1 = sbuf([P, H + S], U8, "picked_scales1")
        scales1 = sbuf([P, H + S], U8, "scales1")
        gather(picked_scales1[:, :H], d_scale_table, k1_list[:])
        gather(picked_scales1[:, H:], x_scale_table, offs_list[:])
        nc.vector.tensor_copy(
            scales1[:, :H].rearrange("p (t m) -> p m t", t=PACK),
            picked_scales1[:, :H].rearrange("p (m t) -> p m t", t=PACK),
        )
        nc.vector.tensor_copy(scales1[:, H:].bitcast(I32), picked_scales1[:, H:].bitcast(I32))
        place_scale_rows(scales1, scales1, range(1, 4))
        n5_list = load_list(n5, "n5_list")
        n3_list = load_list(n3, "n3_list")
        n4_list = load_list(n4, "n4_list")

        picked_k1 = sbuf([P, H], U32, "picked_k1")
        dealt_k1 = sbuf([P, H], U32, "dealt_k1")
        picked_x = sbuf([P, S], U32, "picked_x")
        halves = [slice(0, S // 2), slice(S // 2, S)]
        whole = slice(0, S)
        half_list = S // 2 // 16

        def entries(offsets, cols):
            return offsets[:, cols.start // 16 : cols.stop // 16]

        gather(picked_k1[:], d_word_table, k1_list[:])
        by_tile = picked_k1[:].rearrange("p (m t) -> p m t", t=PACK)
        gather(picked_x[:, halves[0]], x_word_table, entries(offs_list, halves[0]))
        nc.vector.tensor_copy(dealt_k1[:, :P], by_tile[:, :, 0])
        gather(picked_x[:, halves[1]], x_word_table, entries(offs_list, halves[1]))
        nc.vector.tensor_copy(dealt_k1[:, P:].rearrange("p (t m) -> p m t", t=PACK - 1), by_tile[:, :, 1:])

        pieces1 = [(0, halves[0]), (1, whole), (0, halves[1]), (2, whole), (3, whole)]
        h = [sbuf([P, S], F32, "h_%d" % t) for t in range(TILES)]
        ds = [sbuf([P, 2 * S], F32, "ds_%d" % t) for t in range(TILES)]
        for i, (t, cols) in enumerate(pieces1):
            rows = slice(t * P, (t + 1) * P)
            acc = psum.tile([P, cols.stop - cols.start], F32, name="h_psum%d" % i, tag="bank%d" % i)
            nc.tensor.matmul_mx(
                out=acc[:],
                lhsT=dealt_k1[:, rows].bitcast(FP8X4),
                lhsT_scale=scales1[:, rows],
                rhs=picked_x[:, cols].bitcast(FP8X4),
                rhs_scale=scales1[:, H:][:, cols],
                start=True,
                stop=True,
            )
            if i == 0:
                nc.scalar.activation(h[t][:, cols], acc[:], COPY, scale=SIXTEENTH)
            else:
                nc.vector.tensor_scalar(h[t][:, cols], acc[:], sixteenth[:], None, ALU.mult)
        for t, cols in pieces1:
            scatter(ds[t], entries(n1_list, cols), h[t][:, cols])

        picked_scales2 = sbuf([P, 2 * H + S], U8, "picked_scales2", tag="sixteenth")
        gather(picked_scales2[:, :H], d_scale_table, k3_list[:])
        gather(picked_scales2[:, H : 2 * H], d_scale_table, k2_list[:])
        gather(picked_scales2[:, 2 * H :], x_scale_table, two_list[:])
        place_scale_rows(scales2, picked_scales2, range(4))
        picked_two = sbuf([P, S], U32, "picked_two", tag="x_scale_table")
        gather(picked_two[:], x_word_table, two_list[:])
        early = sbuf([P, 2, S], F32, "early", tag="x_word_table")
        st = [early[:, 0, :], early[:, 1, :]]
        for t in range(2):
            nc.vector.tensor_tensor(st[t], h[t][:], ds[t][:, :S], ALU.max)
        picked2 = sbuf([P, 2 * H], U32, "picked2", tag="ds_1")
        gather(picked2[:, :H], d_word_table, k3_list[:])
        gather(picked2[:, H:], d_word_table, k2_list[:])
        late = sbuf([P, 2 + TILES, S], F32, "late", tag="d_word_table")
        st = st + [late[:, 0, :], late[:, 1, :]]
        diff = [late[:, 2 + t, :] for t in range(TILES)]
        for t in range(2, TILES):
            nc.vector.tensor_tensor(st[t], h[t][:], ds[t][:, :S], ALU.max)

        pieces = [(0, cols) for cols in halves] + [(t, slice(0, S)) for t in range(1, TILES)]
        banks = ["bank5", "bank6", "bank7", "bank0", "bank1"]
        h2_psum = [
            psum.tile([P, cols.stop - cols.start], F32, name="h2_psum_%d" % i, tag=banks[i])
            for i, (t, cols) in enumerate(pieces)
        ]
        for i, (t, cols) in enumerate(pieces):
            rows = slice(t * P, (t + 1) * P)
            nc.tensor.matmul_mx(
                out=h2_psum[i][:],
                lhsT=picked2[:, rows].bitcast(FP8X4),
                lhsT_scale=scales2[:, rows],
                rhs=picked_two[:, cols].bitcast(FP8X4),
                rhs_scale=scales2[:, 2 * H :][:, cols],
                start=True,
                stop=False,
            )

        ds2 = [sbuf([P, 2 * S], F32, "ds2_%d" % t) for t in range(TILES)]
        z = sbuf([P, S, PACK], BF16, "z")
        z_words = sbuf([P, S], U32, "z_words")
        z_scales = sbuf([P, S], U8, "z_scales")
        for t in range(TILES):
            scatter(ds2[t], n2_list[:], st[t])
            nc.vector.tensor_scalar(diff[t], st[t], minus_gs[:, t : t + 1], None, ALU.mult)
            for cols in halves if t == TILES - 1 else [whole]:
                nc.vector.scalar_tensor_tensor(
                    z[:, cols, t], ds2[t][:, cols], minus_gs[:, t : t + 1], diff[t][:, cols], ALU.mult, ALU.subtract
                )
        for cols in halves:
            nc.vector.quantize_mx(
                z_words[:, cols].bitcast(FP8X4), z_scales[:, cols], z[:, cols, :].rearrange("p c t -> p (c t)")
            )

        for i, (t, cols) in enumerate(pieces):
            rows = slice(H + t * P, H + (t + 1) * P)
            nc.tensor.matmul_mx(
                out=h2_psum[i][:],
                lhsT=picked2[:, rows].bitcast(FP8X4),
                lhsT_scale=scales2[:, rows],
                rhs=z_words[:, cols].bitcast(FP8X4),
                rhs_scale=z_scales[:, cols],
                start=False,
                stop=True,
            )
        nc.scalar.activation(h2[0][:, halves[0]], h2_psum[0][:], COPY, scale=SIXTEENTH)
        for i, (t, cols) in list(enumerate(pieces))[1:]:
            nc.vector.tensor_scalar(h2[t][:, cols], h2_psum[i][:], SIXTEENTH, None, ALU.mult)

        page = [sbuf([P, U], F32, "page_%d" % t) for t in range(TILES)]
        nw = [sbuf([P, S], F32, "nw_%d" % t) for t in range(TILES)]

        def finish(t):
            scatter(page[t], n4_list[:], nw[t][:])
            nc.sync.dma_start(out[t * P : (t + 1) * P, :], page[t][:])

        scatter(page[0], n3_list[:, :half_list], h2[0][:, halves[0]])
        for t in range(TILES):
            fetched = sbuf([P, S], F32, "fetched_%d" % t)
            nc.scalar.activation(fetched[:], h2[t][:].indirect(n5_list[:]), COPY)
            nc.vector.tensor_tensor(nw[t][:], h2[t][:, :S], fetched[:], ALU.subtract)
            if t == 0:
                scatter(page[0], n3_list[:, half_list:], h2[0][:, halves[1]])
            else:
                scatter(page[t], n3_list[:], h2[t][:, :S])
                finish(t - 1)
        finish(TILES - 1)
